import numpy as np
import ml_dtypes


def mxq(x, axis, fmt="e4m3"):
    dtype, down = {"e4m3": (ml_dtypes.float8_e4m3fn, 7), "e5m2": (ml_dtypes.float8_e5m2, 14)}[fmt]
    v = np.moveaxis(np.asarray(x, np.float32).astype(ml_dtypes.bfloat16).astype(np.float64), axis, -1)
    blocks = v.reshape(v.shape[:-1] + (-1, 32))
    amax = np.abs(blocks).max(-1, keepdims=True)
    byte = np.maximum(np.where(amax > 0, np.frexp(amax)[1] - 1 + 127, 0) - down, 1)
    scale = np.exp2(byte - 127.0)
    codes = (blocks / scale).astype(np.float32).astype(dtype).astype(np.float64)
    return np.moveaxis((codes * scale).reshape(v.shape), -1, axis)


WIDE = False


def mx_kscale(k):
    if not WIDE:
        return np.ones(k)
    levels = np.array([10, -10, 5, -5, 0])
    if k % 512:
        return np.exp2(np.random.permutation(np.resize(levels, k // 32))).repeat(32)
    a = np.empty((k // 512, 16))
    for p in range(k // 512):
        a[p, :8] = np.random.permutation(np.resize(levels, 8))
        for g in range(8):
            far = levels[np.abs(levels - a[p, g]) >= 10]
            a[p, g + 8] = far[np.random.randint(len(far))]
    return np.exp2(a.ravel()).repeat(32)


def f64(x):
    return np.asarray(x).astype(np.float64)


def striped8(idx):
    return np.concatenate([v.reshape(-1, 16).T for v in idx]).astype(np.uint16)


def unstriped8(offs):
    return np.stack([offs[16 * g:16 * g + 16].T.reshape(-1) for g in range(8)]).astype(np.int64)


E2M1 = np.array([0.0, 0.5, 1.0, 1.5, 2.0, 3.0, 4.0, 6.0, -0.0, -0.5, -1.0, -1.5, -2.0, -3.0, -4.0, -6.0])


def pack_weight(w, fmt):
    k, n = w.shape
    w = f64(np.asarray(w, np.float32).astype(ml_dtypes.bfloat16)).reshape(k // 32, 32, n)
    amax = np.abs(w).max(1)
    if fmt == "e4m3":
        byte = np.frexp(amax)[1] - 1 + 127 - 7
    else:
        mant, ex = np.frexp(amax / 6.0)
        byte = np.where(mant > 0.5, ex, ex - 1) + 127
    byte = np.clip(np.where(amax > 0, byte, 1), 1, 254)
    scaled = (w * np.exp2(127.0 - byte)[:, None, :]).reshape(k, n).astype(np.float32)
    by_word = np.ascontiguousarray(scaled.reshape(k // 512, 128, 4, n).transpose(0, 1, 3, 2))
    if fmt == "e4m3":
        words = by_word.astype(ml_dtypes.float8_e4m3fn).view(np.uint8)
    else:
        c = by_word.astype(ml_dtypes.float4_e2m1fn).view(np.uint8) & 0xF
        words = (c[..., 0::2] | (c[..., 1::2] << 4)).reshape(k // 512, 128, 2 * n)
    return np.ascontiguousarray(words), np.ascontiguousarray(byte.astype(np.uint8).reshape(k // 512, 16, n))


def unpack_weight(words, scales, fmt):
    g, _, n = scales.shape
    words = np.ascontiguousarray(words).reshape(g, 128, n, -1)
    if fmt == "e4m3":
        vals = words.view(ml_dtypes.float8_e4m3fn).astype(np.float64)
    else:
        nib = np.empty((g, 128, n, 4), np.uint8)
        nib[..., 0::2] = words & 0xF
        nib[..., 1::2] = words >> 4
        vals = E2M1[nib]
    vals = vals * np.repeat(np.exp2(scales.astype(np.float64) - 127.0), 8, axis=1)[..., None]
    return vals.transpose(0, 1, 3, 2).reshape(g * 512, n)


K, M, T, S = 1536, 512, 512, 256


def setup_inputs():
    n = np.random.standard_normal
    s = mx_kscale(K)[:, None]
    p_w = pack_weight(n((K, M)) / np.sqrt(K) / s, "e2m1")
    return {
        "x": (n((K, S)) * s).astype(np.float32),
        "w_words": p_w[0],
        "w_scales": p_w[1],
        "b": (0.3 * n(512)).astype(np.float32),
        "wgo": np.repeat(np.random.uniform(0.5, 2.0, (8, S)), 16, axis=0).astype(np.float32),
        "offs": striped8(np.stack([np.random.permutation(T)[:S] for _ in range(8)])),
    }


def reference(x, w_words, w_scales, b, wgo, offs):
    x_ = mxq(f64(x), 0, "e4m3")
    w_ = unpack_weight(w_words, w_scales, "e2m1")
    y = w_.T @ x_
    place = unstriped8(offs)[np.arange(M) % 128 // 16]
    out = np.zeros((M, T))
    out[np.arange(M)[:, None], place] = f64(wgo)[np.arange(M) % 128] * (y + f64(b)[:, None])
    return out

@@ -1,0 +1,121 @@
+from contextlib import ExitStack
+
+import concourse.mybir as mybir
+
+F32 = mybir.dt.float32
+BF16 = mybir.dt.bfloat16
+I32 = mybir.dt.int32
+U32 = mybir.dt.uint32
+U16 = mybir.dt.uint16
+U8 = mybir.dt.uint8
+E4M3X4 = mybir.dt.float8_e4m3fn_x4
+E2M1X4 = mybir.dt.float4_e2m1fn_x4
+IDENTITY = mybir.ActivationFunctionType.Identity
+MULT = mybir.AluOpType.mult
+
+K, M, T, S = 1536, 512, 512, 256
+P = 128
+PACK = 4
+PASSES = K // (P * PACK)
+BLOCKS = M // P
+HALF = S // 2
+FLOPS = 2 * K * M * S
+
+
+def tile_list_hscat_bias_kernel(tc, x, w_words, w_scales, b, wgo, offs, out):
+    nc = tc.nc
+    with ExitStack() as ctx:
+        keep = ctx.enter_context(tc.tile_pool(name="keep", bufs=1))
+        psum = ctx.enter_context(tc.psum_pool(name="psum", bufs=1))
+
+        offs_t = keep.tile([P, S // 16], U16, name="offs_t")
+        w_t = keep.tile([P, PASSES, 2 * M], U8, name="w_t", align_bytes=64)
+        ws_t = keep.tile([P, PASSES, M], U8, name="ws_t", align_bytes=64)
+        wgo_t = keep.tile([P, S], F32, name="wgo_t")
+        b_rows = keep.tile([P, P], F32, name="b_rows", align_bytes=64)
+        b_cols = keep.tile([P, P], F32, name="b_cols", align_bytes=64)
+        warm_in = keep.tile([P, 1], F32, name="warm_in")
+        warm_out = keep.tile([P, 1], F32, name="warm_out")
+        windows = [keep.tile([P, T], F32, name=f"window{m}") for m in range(BLOCKS)]
+        raw = [[keep.tile([P, PACK, HALF], F32, name=f"raw{h}_{a}") for a in range(PASSES)] for h in range(2)]
+        grouped = [[keep.tile([P, HALF, PACK], BF16, name=f"grouped{h}_{a}", align_bytes=64) for a in range(PASSES)] for h in range(2)]
+        codes = [[keep.tile([P, HALF], U32, name=f"codes{h}_{a}", align_bytes=64) for a in range(PASSES)] for h in range(2)]
+        scales = [[keep.tile([P, HALF], U8, name=f"scales{h}_{a}", align_bytes=64) for a in range(PASSES)] for h in range(2)]
+        biased = [[keep.tile([P, HALF], F32, name=f"biased{h}_{m}") for m in range(BLOCKS)] for h in range(2)]
+        sums = [[psum.tile([P, HALF], F32, name=f"sums{h}_{m}") for m in range(BLOCKS)] for h in range(2)]
+
+        def load_x(h, a):
+            rows = x[a * P * PACK : (a + 1) * P * PACK, h * HALF : (h + 1) * HALF]
+            nc.sync.dma_start(raw[h][a][:], rows.rearrange("(p j) c -> p j c", j=PACK))
+
+        def interleave(copy, h, a, lo, hi):
+            copy(out=grouped[h][a][:, lo:hi, :], in_=raw[h][a][:, :, lo:hi].rearrange("p j c -> p c j"))
+
+        def quantize(h, a):
+            nc.vector.quantize_mx(
+                out=codes[h][a][:].bitcast(E4M3X4),
+                scales=scales[h][a][:],
+                in_=grouped[h][a][:].rearrange("p c j -> p (c j)"),
+            )
+
+        def multiply(h, a, m):
+            nc.tensor.matmul_mx(
+                out=sums[h][m][:],
+                lhsT=w_t[:, a, m * 2 * P : (m + 1) * 2 * P].bitcast(E2M1X4),
+                lhsT_scale=ws_t[:, a, m * P : (m + 1) * P],
+                rhs=codes[h][a][:].bitcast(E4M3X4),
+                rhs_scale=scales[h][a][:],
+                start=(a == 0),
+                stop=(a == PASSES - 1),
+            )
+
+        def add_bias(h, m):
+            nc.scalar.activation(biased[h][m][:], sums[h][m][:], IDENTITY, bias=b_cols[:, 32 * m : 32 * m + 1])
+
+        def scatter(h, m):
+            places = offs_t[:, h * HALF // 16 : (h + 1) * HALF // 16]
+            nc.vector.tensor_tensor(windows[m][:].indirect(places), biased[h][m][:], wgo_t[:, h * HALF : (h + 1) * HALF], MULT)
+
+        nc.vector.memset(warm_in[:], 0.0)
+        nc.scalar.activation(warm_out[:], warm_in[:], IDENTITY)
+        nc.vector.memset(ws_t[:].bitcast(I32), 0)
+        nc.vector.memset(b_rows[:], 0.0)
+        ws_in = w_scales.bitcast(I32).rearrange("a (q r) n -> r q a n", r=4)
+        for r in range(4):
+            nc.scalar.dma_start(ws_t[r:P:32, :, :].bitcast(I32), ws_in[r])
+        for a in range(PASSES):
+            load_x(0, a)
+        nc.sync.dma_start(w_t[:].bitcast(I32), w_words.bitcast(I32).rearrange("a p c -> p a c"))
+        nc.sync.dma_start(b_rows[0:P:32, :].rearrange("q (m i) -> q m i", m=BLOCKS), b.rearrange("(m q i) -> q m i", m=BLOCKS, q=4))
+        nc.sync.dma_start(offs_t[:], offs)
+        nc.sync.dma_start(wgo_t[:], wgo)
+        for a in range(PASSES):
+            load_x(1, a)
+        for m in range(BLOCKS):
+            nc.vector.memset(windows[m][:], 0.0)
+
+        interleave(nc.vector.tensor_copy, 0, 0, 0, HALF)
+        quantize(0, 0)
+        interleave(nc.scalar.copy, 0, 1, 0, HALF)
+        quantize(0, 1)
+        interleave(nc.vector.tensor_copy, 0, 2, 0, 80)
+        interleave(nc.scalar.copy, 0, 2, 80, HALF)
+        quantize(0, 2)
+        nc.vector.transpose(b_cols[:], b_rows[:])
+        for m in range(BLOCKS):
+            for a in range(PASSES):
+                multiply(0, a, m)
+            add_bias(0, m)
+        for m in range(BLOCKS - 1):
+            scatter(0, m)
+        for a in range(PASSES):
+            interleave(nc.scalar.copy, 1, a, 0, HALF)
+            quantize(1, a)
+        scatter(0, BLOCKS - 1)
+        for a in range(PASSES):
+            for m in range(BLOCKS):
+                multiply(1, a, m)
+        for m in range(BLOCKS):
+            add_bias(1, m)
+            scatter(1, m)
+            nc.sync.dma_start(out[m * P : (m + 1) * P, :], windows[m][:])

@@ -37,19 +37,22 @@ def tile_list_hscat_bias_kernel(tc, x, w_words, w_scales, b, wgo, offs, out):
         warm_in = keep.tile([P, 1], F32, name="warm_in")
         warm_out = keep.tile([P, 1], F32, name="warm_out")
         windows = [keep.tile([P, T], F32, name=f"window{m}") for m in range(BLOCKS)]
-        raw = [[keep.tile([P, PACK, HALF], F32, name=f"raw{h}_{a}") for a in range(PASSES)] for h in range(2)]
+        raw_all = keep.tile([P, PASSES, PACK, S], F32, name="raw_all")
         grouped = [[keep.tile([P, HALF, PACK], BF16, name=f"grouped{h}_{a}", align_bytes=64) for a in range(PASSES)] for h in range(2)]
         codes = [[keep.tile([P, HALF], U32, name=f"codes{h}_{a}", align_bytes=64) for a in range(PASSES)] for h in range(2)]
         scales = [[keep.tile([P, HALF], U8, name=f"scales{h}_{a}", align_bytes=64) for a in range(PASSES)] for h in range(2)]
         biased = [[keep.tile([P, HALF], F32, name=f"biased{h}_{m}") for m in range(BLOCKS)] for h in range(2)]
         sums = [[psum.tile([P, HALF], F32, name=f"sums{h}_{m}") for m in range(BLOCKS)] for h in range(2)]
 
-        def load_x(h, a):
-            rows = x[a * P * PACK : (a + 1) * P * PACK, h * HALF : (h + 1) * HALF]
-            nc.sync.dma_start(raw[h][a][:], rows.rearrange("(p j) c -> p j c", j=PACK))
+        def load_x(first, last):
+            rows = x[first * P * PACK : last * P * PACK, :].rearrange("(a p j) c -> p a (j c)", p=P, j=PACK)
+            nc.sync.dma_start(raw_all[:, first:last, :, :].rearrange("p a j c -> p a (j c)"), rows)
 
-        def interleave(copy, h, a, lo, hi):
-            copy(out=grouped[h][a][:, lo:hi, :], in_=raw[h][a][:, :, lo:hi].rearrange("p j c -> p c j"))
+        def load_w(lo, hi):
+            nc.sync.dma_start(w_t[:, :, 2 * lo : 2 * hi].bitcast(I32), w_words[:, :, 2 * lo : 2 * hi].bitcast(I32).rearrange("a p c -> p a c"))
+
+        def interleave(copy, a, lo, hi):
+            copy(out=grouped[lo // HALF][a][:, lo % HALF : lo % HALF + hi - lo, :], in_=raw_all[:, a, :, lo:hi].rearrange("p j c -> p c j"))
 
         def quantize(h, a):
             nc.vector.quantize_mx(
@@ -76,46 +79,39 @@ def tile_list_hscat_bias_kernel(tc, x, w_words, w_scales, b, wgo, offs, out):
             places = offs_t[:, h * HALF // 16 : (h + 1) * HALF // 16]
             nc.vector.tensor_tensor(windows[m][:].indirect(places), biased[h][m][:], wgo_t[:, h * HALF : (h + 1) * HALF], MULT)
 
-        nc.vector.memset(warm_in[:], 0.0)
+        nc.gpsimd.memset(warm_in[:], 0.0)
         nc.scalar.activation(warm_out[:], warm_in[:], IDENTITY)
-        nc.vector.memset(ws_t[:].bitcast(I32), 0)
         nc.vector.memset(b_rows[:], 0.0)
         ws_in = w_scales.bitcast(I32).rearrange("a (q r) n -> r q a n", r=4)
         for r in range(4):
             nc.scalar.dma_start(ws_t[r:P:32, :, :].bitcast(I32), ws_in[r])
-        for a in range(PASSES):
-            load_x(0, a)
-        nc.sync.dma_start(w_t[:].bitcast(I32), w_words.bitcast(I32).rearrange("a p c -> p a c"))
+        load_x(0, 2)
         nc.sync.dma_start(b_rows[0:P:32, :].rearrange("q (m i) -> q m i", m=BLOCKS), b.rearrange("(m q i) -> q m i", m=BLOCKS, q=4))
+        load_x(2, 3)
+        load_w(0, M // 2)
         nc.sync.dma_start(offs_t[:], offs)
         nc.sync.dma_start(wgo_t[:], wgo)
-        for a in range(PASSES):
-            load_x(1, a)
+        load_w(M // 2, M)
         for m in range(BLOCKS):
             nc.vector.memset(windows[m][:], 0.0)
 
-        interleave(nc.vector.tensor_copy, 0, 0, 0, HALF)
-        quantize(0, 0)
-        interleave(nc.scalar.copy, 0, 1, 0, HALF)
-        quantize(0, 1)
-        interleave(nc.vector.tensor_copy, 0, 2, 0, 80)
-        interleave(nc.scalar.copy, 0, 2, 80, HALF)
-        quantize(0, 2)
+        for a in range(2):
+            interleave(nc.vector.tensor_copy, a, 0, HALF)
+            interleave(nc.scalar.copy, a, HALF, S)
+        for a in range(2):
+            quantize(0, a)
+        interleave(nc.vector.tensor_copy, 2, 0, HALF)
         nc.vector.transpose(b_cols[:], b_rows[:])
-        for m in range(BLOCKS):
-            for a in range(PASSES):
-                multiply(0, a, m)
-            add_bias(0, m)
-        for m in range(BLOCKS - 1):
-            scatter(0, m)
+        quantize(0, 2)
+        interleave(nc.scalar.copy, 2, HALF, S)
         for a in range(PASSES):
-            interleave(nc.scalar.copy, 1, a, 0, HALF)
             quantize(1, a)
-        scatter(0, BLOCKS - 1)
-        for a in range(PASSES):
-            for m in range(BLOCKS):
-                multiply(1, a, m)
-        for m in range(BLOCKS):
-            add_bias(1, m)
-            scatter(1, m)
-            nc.sync.dma_start(out[m * P : (m + 1) * P, :], windows[m][:])
+        for m0 in range(0, BLOCKS, 2):
+            for h in range(2):
+                for m in (m0, m0 + 1):
+                    for a in range(PASSES):
+                        multiply(h, a, m)
+                    add_bias(h, m)
+                    scatter(h, m)
+                    if h == 1:
+                        nc.sync.dma_start(out[m * P : (m + 1) * P, :], windows[m][:])

from contextlib import ExitStack

import concourse.mybir as mybir

F32 = mybir.dt.float32
BF16 = mybir.dt.bfloat16
I32 = mybir.dt.int32
U32 = mybir.dt.uint32
U16 = mybir.dt.uint16
U8 = mybir.dt.uint8
E4M3X4 = mybir.dt.float8_e4m3fn_x4
E2M1X4 = mybir.dt.float4_e2m1fn_x4
IDENTITY = mybir.ActivationFunctionType.Identity
MULT = mybir.AluOpType.mult

K, M, T, S = 1536, 512, 512, 256
P = 128
PACK = 4
PASSES = K // (P * PACK)
BLOCKS = M // P
HALF = S // 2
FLOPS = 2 * K * M * S


def tile_list_hscat_bias_kernel(tc, x, w_words, w_scales, b, wgo, offs, out):
    nc = tc.nc
    with ExitStack() as ctx:
        keep = ctx.enter_context(tc.tile_pool(name="keep", bufs=1))
        psum = ctx.enter_context(tc.psum_pool(name="psum", bufs=1))

        offs_t = keep.tile([P, S // 16], U16, name="offs_t")
        w_t = keep.tile([P, PASSES, 2 * M], U8, name="w_t", align_bytes=64)
        ws_t = keep.tile([P, PASSES, M], U8, name="ws_t", align_bytes=64)
        wgo_t = keep.tile([P, S], F32, name="wgo_t")
        b_rows = keep.tile([P, P], F32, name="b_rows", align_bytes=64)
        b_cols = keep.tile([P, P], F32, name="b_cols", align_bytes=64)
        warm_in = keep.tile([P, 1], F32, name="warm_in")
        warm_out = keep.tile([P, 1], F32, name="warm_out")
        windows = [keep.tile([P, T], F32, name=f"window{m}") for m in range(BLOCKS)]
        raw_all = keep.tile([P, PASSES, PACK, S], F32, name="raw_all")
        grouped = [[keep.tile([P, HALF, PACK], BF16, name=f"grouped{h}_{a}", align_bytes=64) for a in range(PASSES)] for h in range(2)]
        codes = [[keep.tile([P, HALF], U32, name=f"codes{h}_{a}", align_bytes=64) for a in range(PASSES)] for h in range(2)]
        scales = [[keep.tile([P, HALF], U8, name=f"scales{h}_{a}", align_bytes=64) for a in range(PASSES)] for h in range(2)]
        biased = [[keep.tile([P, HALF], F32, name=f"biased{h}_{m}") for m in range(BLOCKS)] for h in range(2)]
        sums = [[psum.tile([P, HALF], F32, name=f"sums{h}_{m}") for m in range(BLOCKS)] for h in range(2)]

        def load_x(first, last):
            rows = x[first * P * PACK : last * P * PACK, :].rearrange("(a p j) c -> p a (j c)", p=P, j=PACK)
            nc.sync.dma_start(raw_all[:, first:last, :, :].rearrange("p a j c -> p a (j c)"), rows)

        def load_w(lo, hi):
            nc.sync.dma_start(w_t[:, :, 2 * lo : 2 * hi].bitcast(I32), w_words[:, :, 2 * lo : 2 * hi].bitcast(I32).rearrange("a p c -> p a c"))

        def interleave(copy, a, lo, hi):
            copy(out=grouped[lo // HALF][a][:, lo % HALF : lo % HALF + hi - lo, :], in_=raw_all[:, a, :, lo:hi].rearrange("p j c -> p c j"))

        def quantize(h, a):
            nc.vector.quantize_mx(
                out=codes[h][a][:].bitcast(E4M3X4),
                scales=scales[h][a][:],
                in_=grouped[h][a][:].rearrange("p c j -> p (c j)"),
            )

        def multiply(h, a, m):
            nc.tensor.matmul_mx(
                out=sums[h][m][:],
                lhsT=w_t[:, a, m * 2 * P : (m + 1) * 2 * P].bitcast(E2M1X4),
                lhsT_scale=ws_t[:, a, m * P : (m + 1) * P],
                rhs=codes[h][a][:].bitcast(E4M3X4),
                rhs_scale=scales[h][a][:],
                start=(a == 0),
                stop=(a == PASSES - 1),
            )

        def add_bias(h, m):
            nc.scalar.activation(biased[h][m][:], sums[h][m][:], IDENTITY, bias=b_cols[:, 32 * m : 32 * m + 1])

        def scatter(h, m):
            places = offs_t[:, h * HALF // 16 : (h + 1) * HALF // 16]
            nc.vector.tensor_tensor(windows[m][:].indirect(places), biased[h][m][:], wgo_t[:, h * HALF : (h + 1) * HALF], MULT)

        nc.gpsimd.memset(warm_in[:], 0.0)
        nc.scalar.activation(warm_out[:], warm_in[:], IDENTITY)
        nc.vector.memset(b_rows[:], 0.0)
        ws_in = w_scales.bitcast(I32).rearrange("a (q r) n -> r q a n", r=4)
        for r in range(4):
            nc.scalar.dma_start(ws_t[r:P:32, :, :].bitcast(I32), ws_in[r])
        load_x(0, 2)
        nc.sync.dma_start(b_rows[0:P:32, :].rearrange("q (m i) -> q m i", m=BLOCKS), b.rearrange("(m q i) -> q m i", m=BLOCKS, q=4))
        load_x(2, 3)
        load_w(0, M // 2)
        nc.sync.dma_start(offs_t[:], offs)
        nc.sync.dma_start(wgo_t[:], wgo)
        load_w(M // 2, M)
        for m in range(BLOCKS):
            nc.vector.memset(windows[m][:], 0.0)

        for a in range(2):
            interleave(nc.vector.tensor_copy, a, 0, HALF)
            interleave(nc.scalar.copy, a, HALF, S)
        for a in range(2):
            quantize(0, a)
        interleave(nc.vector.tensor_copy, 2, 0, HALF)
        nc.vector.transpose(b_cols[:], b_rows[:])
        quantize(0, 2)
        interleave(nc.scalar.copy, 2, HALF, S)
        for a in range(PASSES):
            quantize(1, a)
        for m0 in range(0, BLOCKS, 2):
            for h in range(2):
                for m in (m0, m0 + 1):
                    for a in range(PASSES):
                        multiply(h, a, m)
                    add_bias(h, m)
                    scatter(h, m)
                    if h == 1:
                        nc.sync.dma_start(out[m * P : (m + 1) * P, :], windows[m][:])
